import numpy as np
import ml_dtypes


def mxq(x, axis, fmt="e4m3"):
    dtype, down = {"e4m3": (ml_dtypes.float8_e4m3fn, 7), "e5m2": (ml_dtypes.float8_e5m2, 14)}[fmt]
    v = np.moveaxis(np.asarray(x, np.float32).astype(ml_dtypes.bfloat16).astype(np.float64), axis, -1)
    blocks = v.reshape(v.shape[:-1] + (-1, 32))
    amax = np.abs(blocks).max(-1, keepdims=True)
    byte = np.maximum(np.where(amax > 0, np.frexp(amax)[1] - 1 + 127, 0) - down, 1)
    scale = np.exp2(byte - 127.0)
    codes = (blocks / scale).astype(np.float32).astype(dtype).astype(np.float64)
    return np.moveaxis((codes * scale).reshape(v.shape), -1, axis)


WIDE = False


def mx_kscale(k):
    if not WIDE:
        return np.ones(k)
    levels = np.array([10, -10, 5, -5, 0])
    if k % 512:
        return np.exp2(np.random.permutation(np.resize(levels, k // 32))).repeat(32)
    a = np.empty((k // 512, 16))
    for p in range(k // 512):
        a[p, :8] = np.random.permutation(np.resize(levels, 8))
        for g in range(8):
            far = levels[np.abs(levels - a[p, g]) >= 10]
            a[p, g + 8] = far[np.random.randint(len(far))]
    return np.exp2(a.ravel()).repeat(32)


def f64(x):
    return np.asarray(x).astype(np.float64)


def striped(idx):
    return np.tile(idx.reshape(-1, 16).T, (8, 1)).astype(np.uint16)


def unstriped(offs):
    return offs[:16].T.reshape(-1).astype(np.int64)


K, T, E, C, N = 1024, 512, 8, 128, 256


def by_expert(wq, xq):
    return np.concatenate([wq[e].T @ xq[:, e * C:(e + 1) * C] for e in range(E)], axis=1)


def setup_inputs():
    n = np.random.standard_normal
    s = mx_kscale(K)[:, None]
    first = np.random.permutation(np.repeat(np.arange(E), T // E))
    second = (first + 1 + np.random.permutation(np.repeat(np.arange(E - 1), -(-T // (E - 1)))[:T])) % E
    while np.bincount(second, minlength=E).max() != T // E:
        load = np.bincount(second, minlength=E); hi, lo = int(load.argmax()), int(load.argmin())
        t = np.flatnonzero((second == hi) & (first != lo))[0]; second[t] = lo
    slot_token = np.empty(E * C, np.int64); pos = np.empty((2, T), np.int64); fill = np.zeros(E, np.int64)
    place = np.stack([np.random.permutation(C) for _ in range(E)])
    for r, deal in enumerate((first, second)):
        for t in np.random.permutation(T):
            e = deal[t]; j = e * C + place[e, fill[e]]; fill[e] += 1; slot_token[j] = t; pos[r, t] = j
    g = np.random.uniform(0.2, 0.8, T)
    return {
        "xT": (n((K, T)) * s).astype(np.float32),
        "w": (n((E, K, N)) / np.sqrt(K) / s[None]).astype(np.float32),
        "gate": np.stack([np.tile(g, (N, 1)), np.tile(1.0 - g, (N, 1))]).astype(np.float32),
        "offs": striped(slot_token),
        "pos1": striped(pos[0]),
        "pos2": striped(pos[1]),
    }


def reference(xT, w, gate, offs, pos1, pos2):
    idx = unstriped(offs)
    xq = mxq(f64(xT)[:, idx], 0, "e4m3")
    y = by_expert(mxq(f64(w), 1, "e4m3"), xq)
    return f64(gate[0]) * y[:, unstriped(pos1)] + f64(gate[1]) * y[:, unstriped(pos2)]

@@ -1,0 +1,180 @@
+from contextlib import ExitStack
+
+import concourse.mybir as mybir
+
+K, T, E, C, N = 1024, 512, 8, 128, 256
+FLOPS = 2 * K * N * E * C
+
+F32 = mybir.dt.float32
+BF16 = mybir.dt.bfloat16
+I32 = mybir.dt.int32
+U32 = mybir.dt.uint32
+U16 = mybir.dt.uint16
+U8 = mybir.dt.uint8
+FP8X4 = mybir.dt.float8_e4m3fn_x4
+MULT = mybir.AluOpType.mult
+ADD = mybir.AluOpType.add
+
+P = 128
+PACK = 4
+RUN = 4
+PASSES = K // (P * PACK)
+NB = N // P
+SLOTS = E * C
+WIN = 2 * SLOTS
+X_CHUNK = (512, 512)
+X0_V = 352
+LAST_V = 160
+EW = PASSES * N
+W_ENGINE = ["s", "s", "s", "s", "v", "s", "sv"]
+BANKS = [(0, 1, 4, 5), (2, 3, 6, 7)]
+
+
+def tile_routed_moe_kernel(tc, xT, w, gate, offs, pos1, pos2, out):
+    nc = tc.nc
+
+    def move(engine, dst, src):
+        if engine == "s":
+            nc.scalar.copy(out=dst, in_=src)
+        elif engine == "v":
+            nc.vector.tensor_copy(out=dst, in_=src)
+        else:
+            nc.gpsimd.tensor_scalar(out=dst, in0=src, scalar1=1.0, scalar2=0.0, op0=MULT, op1=ADD)
+
+    with ExitStack() as ctx:
+        lists = ctx.enter_context(tc.tile_pool(name="lists", bufs=1))
+        keep = ctx.enter_context(tc.tile_pool(name="keep", bufs=1))
+        psum = ctx.enter_context(tc.psum_pool(name="psum", bufs=1))
+
+        offs_t = lists.tile([P, SLOTS // 16], U16, name="offs_t")
+        pos1_t = lists.tile([P, T // 16], U16, name="pos1_t")
+        pos2_t = lists.tile([P, T // 16], U16, name="pos2_t")
+
+        x_view = xT.rearrange("(a p j) t -> a p j t", p=P, j=PACK)
+        xraw = {}
+        for a in range(PASSES):
+            for c in range(T // X_CHUNK[a]):
+                t_ = keep.tile([P, PACK, X_CHUNK[a]], F32, name="xraw%d_%d" % (a, c))
+                nc.sync.dma_start(t_[:], x_view[a, :, :, c * X_CHUNK[a]:(c + 1) * X_CHUNK[a]])
+                xraw[(a, c)] = t_
+            if a == 0:
+                nc.sync.dma_start(offs_t[:], offs)
+        wraw = []
+        for e in range(E):
+            t_ = keep.tile([P, PASSES, PACK * N], F32, name="wraw%d" % e)
+            src = w[e].rearrange("(a p j) n -> p a (j n)", p=P, j=PACK)
+            if e < E - 1:
+                nc.sync.dma_start(t_[:], src)
+            else:
+                for a in range(PASSES):
+                    nc.sync.dma_start(t_[:, a, :], src[:, a, :])
+            wraw.append(t_)
+        nc.sync.dma_start(pos1_t[:], pos1)
+        nc.sync.dma_start(pos2_t[:], pos2)
+        g_t = {}
+        for b in range(NB):
+            for r in range(2):
+                t_ = keep.tile([P, T], F32, name="gate%d%d" % (r, b))
+                nc.sync.dma_start(t_[:], gate[r, b * P:(b + 1) * P, :])
+                g_t[(r, b)] = t_
+
+        warm = keep.tile([P, 1], F32, name="warm")
+        nc.vector.memset(warm[:], 0.0)
+        warm2 = keep.tile([P, 1], F32, name="warm2")
+        nc.scalar.copy(warm2[:], warm[:])
+
+        xq, xsc = [], []
+        for a in range(PASSES):
+            sc = keep.tile([P, WIN], U8, name="xsc%d" % a, align_bytes=64)
+            nc.vector.memset(sc[:].bitcast(I32), 0)
+            xsc.append(sc)
+            q = keep.tile([P, WIN], I32, name="xq%d" % a, align_bytes=64)
+            nc.vector.memset(q[:, T:WIN], 0)
+            xq.append(q)
+        for a in range(PASSES):
+            xg = keep.tile([P, T * PACK], BF16, name="xg%d" % a, align_bytes=64)
+            dst = xg[:].rearrange("p (c i j) -> p c j i", i=RUN, j=PACK)
+            XCH = X_CHUNK[a]
+            for c in range(T // XCH):
+                src = xraw[(a, c)][:].rearrange("p j (c i) -> p c j i", i=RUN)
+                c0 = c * XCH // RUN
+                v = X0_V if a == 0 else 0
+                if v:
+                    nc.vector.tensor_copy(out=dst[:, c0:c0 + v // RUN], in_=src[:, 0:v // RUN])
+                nc.scalar.copy(out=dst[:, c0 + v // RUN:c0 + XCH // RUN], in_=src[:, v // RUN:XCH // RUN])
+                if a == 0:
+                    tc_ = slice(c * XCH, (c + 1) * XCH)
+                    nc.vector.quantize_mx(out=xq[a][:, tc_].bitcast(FP8X4), scales=xsc[a][:, tc_],
+                                          in_=xg[:, c * XCH * PACK:(c + 1) * XCH * PACK])
+            if a > 0:
+                nc.vector.quantize_mx(out=xq[a][:, 0:T].bitcast(FP8X4), scales=xsc[a][:, 0:T], in_=xg[:])
+
+        xgq = [keep.tile([P, SLOTS], U32, name="xgq%d" % a, align_bytes=64) for a in range(PASSES)]
+        xgs = [keep.tile([P, SLOTS], U8, name="xgs%d" % a, align_bytes=64) for a in range(PASSES)]
+        y = [keep.tile([P, SLOTS], F32, name="y%d" % b) for b in range(NB)]
+
+        for a in range(PASSES):
+            nc.vector.tensor_copy(out=xgq[a][:], in_=xq[a][:].bitcast(U32).indirect(offs_t[:]))
+            nc.vector.tensor_copy(out=xgs[a][:], in_=xsc[a][:].indirect(offs_t[:]))
+
+        bank_of = {}
+        for q, experts in enumerate(BANKS):
+            for i, e in enumerate(experts):
+                bank_of[e] = (q, i)
+        ps = {}
+        for q in range(len(BANKS)):
+            for b in range(NB):
+                ps[(q, b)] = psum.tile([P, 4 * C], F32, name="ps%d_%d" % (q, b))
+        for e in range(E):
+            last = e == E - 1
+            wg = keep.tile([P, EW * PACK], BF16, name="wg%d" % e, align_bytes=64)
+            wq = keep.tile([P, EW], U32, name="wq%d" % e, align_bytes=64)
+            ws = keep.tile([P, EW], U8, name="ws%d" % e, align_bytes=64)
+            src = wraw[e][:].rearrange("p a (j c i) -> p a c j i", j=PACK, i=RUN)
+            dst = wg[:].rearrange("p (a c i j) -> p a c j i", a=PASSES, i=RUN, j=PACK)
+            if last:
+                move("v", dst[:, 0], src[:, 0])
+                move("v", dst[:, 1, 0:LAST_V // RUN], src[:, 1, 0:LAST_V // RUN])
+                move("s", dst[:, 1, LAST_V // RUN:N // RUN], src[:, 1, LAST_V // RUN:N // RUN])
+            elif len(W_ENGINE[e]) == PASSES:
+                for a in range(PASSES):
+                    move(W_ENGINE[e][a], dst[:, a], src[:, a])
+            else:
+                move(W_ENGINE[e], dst, src)
+            if last:
+                for a in range(PASSES):
+                    nc.vector.quantize_mx(out=wq[:, a * N:(a + 1) * N].bitcast(FP8X4), scales=ws[:, a * N:(a + 1) * N],
+                                          in_=wg[:, a * N * PACK:(a + 1) * N * PACK])
+            else:
+                nc.vector.quantize_mx(out=wq[:].bitcast(FP8X4), scales=ws[:], in_=wg[:])
+            q, i = bank_of[e]
+            for b in range(NB):
+                acc = ps[(q, b)][:, i * C:(i + 1) * C]
+                for a in range(PASSES):
+                    wc = slice(a * N + b * P, a * N + (b + 1) * P)
+                    xc = slice(e * C, (e + 1) * C)
+                    nc.tensor.matmul_mx(
+                        out=acc,
+                        lhsT=wq[:, wc].bitcast(FP8X4),
+                        lhsT_scale=ws[:, wc],
+                        rhs=xgq[a][:, xc].bitcast(FP8X4),
+                        rhs_scale=xgs[a][:, xc],
+                        start=(a == 0),
+                        stop=(a == PASSES - 1),
+                    )
+                if i == 3:
+                    nc.scalar.copy(out=y[b][:].rearrange("p (h q c) -> p h q c", h=2, q=2)[:, :, q, :],
+                                   in_=ps[(q, b)][:].rearrange("p (h c) -> p h c", h=2))
+
+        for b in range(NB):
+            t1 = keep.tile([P, T], F32, name="t1_%d" % b)
+            t2 = keep.tile([P, T], F32, name="t2_%d" % b)
+            o = keep.tile([P, T], F32, name="o_%d" % b)
+            nc.vector.tensor_tensor(out=t1[:], in0=y[b][:].indirect(pos1_t[:]), in1=g_t[(0, b)][:], op=MULT)
+            nc.vector.tensor_tensor(out=t2[:], in0=y[b][:].indirect(pos2_t[:]), in1=g_t[(1, b)][:], op=MULT)
+            nc.vector.tensor_add(out=o[:], in0=t1[:], in1=t2[:])
+            if b < NB - 1:
+                nc.sync.dma_start(out[b * P:(b + 1) * P, :], o[:])
+            else:
+                nc.sync.dma_start(out[b * P:(b + 1) * P, 0:T // 2], o[:, 0:T // 2])
+                nc.scalar.dma_start(out[b * P:(b + 1) * P, T // 2:T], o[:, T // 2:T])

@@ -17,6 +17,7 @@ ADD = mybir.AluOpType.add
 
 P = 128
 PACK = 4
+ROW0 = 4
 RUN = 4
 PASSES = K // (P * PACK)
 NB = N // P
@@ -27,7 +28,7 @@ X0_V = 352
 LAST_V = 160
 EW = PASSES * N
 W_ENGINE = ["s", "s", "s", "s", "v", "s", "sv"]
-BANKS = [(0, 1, 4, 5), (2, 3, 6, 7)]
+BANKS = [(0, 1, 4, 5), (2, 3, 6), (7,)]
 
 
 def tile_routed_moe_kernel(tc, xT, w, gate, offs, pos1, pos2, out):
@@ -83,11 +84,10 @@ def tile_routed_moe_kernel(tc, xT, w, gate, offs, pos1, pos2, out):
         warm2 = keep.tile([P, 1], F32, name="warm2")
         nc.scalar.copy(warm2[:], warm[:])
 
-        xq, xsc = [], []
+        xq = []
+        xsc = keep.tile([P, WIN], U8, name="xsc", align_bytes=64)
+        nc.vector.memset(xsc[:].bitcast(I32), 0)
         for a in range(PASSES):
-            sc = keep.tile([P, WIN], U8, name="xsc%d" % a, align_bytes=64)
-            nc.vector.memset(sc[:].bitcast(I32), 0)
-            xsc.append(sc)
             q = keep.tile([P, WIN], I32, name="xq%d" % a, align_bytes=64)
             nc.vector.memset(q[:, T:WIN], 0)
             xq.append(q)
@@ -104,18 +104,18 @@ def tile_routed_moe_kernel(tc, xT, w, gate, offs, pos1, pos2, out):
                 nc.scalar.copy(out=dst[:, c0 + v // RUN:c0 + XCH // RUN], in_=src[:, v // RUN:XCH // RUN])
                 if a == 0:
                     tc_ = slice(c * XCH, (c + 1) * XCH)
-                    nc.vector.quantize_mx(out=xq[a][:, tc_].bitcast(FP8X4), scales=xsc[a][:, tc_],
+                    nc.vector.quantize_mx(out=xq[a][:, tc_].bitcast(FP8X4), scales=xsc[ROW0 * a:P, tc_],
                                           in_=xg[:, c * XCH * PACK:(c + 1) * XCH * PACK])
             if a > 0:
-                nc.vector.quantize_mx(out=xq[a][:, 0:T].bitcast(FP8X4), scales=xsc[a][:, 0:T], in_=xg[:])
+                nc.vector.quantize_mx(out=xq[a][:, 0:T].bitcast(FP8X4), scales=xsc[ROW0 * a:P, 0:T], in_=xg[:])
 
         xgq = [keep.tile([P, SLOTS], U32, name="xgq%d" % a, align_bytes=64) for a in range(PASSES)]
-        xgs = [keep.tile([P, SLOTS], U8, name="xgs%d" % a, align_bytes=64) for a in range(PASSES)]
+        xgs = keep.tile([P, SLOTS], U8, name="xgs", align_bytes=64)
         y = [keep.tile([P, SLOTS], F32, name="y%d" % b) for b in range(NB)]
 
-        for a in range(PASSES):
-            nc.vector.tensor_copy(out=xgq[a][:], in_=xq[a][:].bitcast(U32).indirect(offs_t[:]))
-            nc.vector.tensor_copy(out=xgs[a][:], in_=xsc[a][:].indirect(offs_t[:]))
+        nc.vector.tensor_copy(out=xgq[0][:], in_=xq[0][:].bitcast(U32).indirect(offs_t[:]))
+        nc.vector.tensor_copy(out=xgs[:], in_=xsc[:].indirect(offs_t[:]))
+        nc.vector.tensor_copy(out=xgq[1][:], in_=xq[1][:].bitcast(U32).indirect(offs_t[:]))
 
         bank_of = {}
         for q, experts in enumerate(BANKS):
@@ -158,13 +158,18 @@ def tile_routed_moe_kernel(tc, xT, w, gate, offs, pos1, pos2, out):
                         lhsT=wq[:, wc].bitcast(FP8X4),
                         lhsT_scale=ws[:, wc],
                         rhs=xgq[a][:, xc].bitcast(FP8X4),
-                        rhs_scale=xgs[a][:, xc],
+                        rhs_scale=xgs[ROW0 * a:P, xc],
                         start=(a == 0),
                         stop=(a == PASSES - 1),
                     )
-                if i == 3:
-                    nc.scalar.copy(out=y[b][:].rearrange("p (h q c) -> p h q c", h=2, q=2)[:, :, q, :],
-                                   in_=ps[(q, b)][:].rearrange("p (h c) -> p h c", h=2))
+                if e == 5:
+                    nc.scalar.copy(out=y[b][:].rearrange("p (h q c) -> p h q c", h=2, q=2)[:, :, 0, :],
+                                   in_=ps[(0, b)][:].rearrange("p (h c) -> p h c", h=2))
+                elif e == 6:
+                    nc.scalar.copy(out=y[b][:, 2 * C:4 * C], in_=ps[(1, b)][:, 0:2 * C])
+                    nc.scalar.copy(out=y[b][:, 6 * C:7 * C], in_=ps[(1, b)][:, 2 * C:3 * C])
+                elif e == 7:
+                    move("v" if b == 0 else "s", y[b][:, 7 * C:8 * C], ps[(2, b)][:, 0:C])
 
         for b in range(NB):
             t1 = keep.tile([P, T], F32, name="t1_%d" % b)

@@ -25,7 +25,7 @@ SLOTS = E * C
 WIN = 2 * SLOTS
 X_CHUNK = (512, 512)
 X0_V = 352
-LAST_V = 160
+LAST_V = 128
 EW = PASSES * N
 W_ENGINE = ["s", "s", "s", "s", "v", "s", "sv"]
 BANKS = [(0, 1, 4, 5), (2, 3, 6), (7,)]
@@ -142,9 +142,9 @@ def tile_routed_moe_kernel(tc, xT, w, gate, offs, pos1, pos2, out):
             else:
                 move(W_ENGINE[e], dst, src)
             if last:
-                for a in range(PASSES):
-                    nc.vector.quantize_mx(out=wq[:, a * N:(a + 1) * N].bitcast(FP8X4), scales=ws[:, a * N:(a + 1) * N],
-                                          in_=wg[:, a * N * PACK:(a + 1) * N * PACK])
+                for c0, c1 in ((0, N), (N, N + P), (N + P, 2 * N)):
+                    nc.vector.quantize_mx(out=wq[:, c0:c1].bitcast(FP8X4), scales=ws[:, c0:c1],
+                                          in_=wg[:, c0 * PACK:c1 * PACK])
             else:
                 nc.vector.quantize_mx(out=wq[:].bitcast(FP8X4), scales=ws[:], in_=wg[:])
             q, i = bank_of[e]

@@ -27,7 +27,8 @@ X_CHUNK = (512, 512)
 X0_V = 352
 LAST_V = 128
 EW = PASSES * N
-W_ENGINE = ["s", "s", "s", "s", "v", "s", "sv"]
+FIRST_BY_PASS = 5
+W_ENGINE = ["s", "s", "s", "s", "v", "sv", "sv"]
 BANKS = [(0, 1, 4, 5), (2, 3, 6), (7,)]
 
 
@@ -64,7 +65,7 @@ def tile_routed_moe_kernel(tc, xT, w, gate, offs, pos1, pos2, out):
         for e in range(E):
             t_ = keep.tile([P, PASSES, PACK * N], F32, name="wraw%d" % e)
             src = w[e].rearrange("(a p j) n -> p a (j n)", p=P, j=PACK)
-            if e < E - 1:
+            if e < FIRST_BY_PASS:
                 nc.sync.dma_start(t_[:], src)
             else:
                 for a in range(PASSES):

@@ -28,7 +28,7 @@ X0_V = 352
 LAST_V = 128
 EW = PASSES * N
 FIRST_BY_PASS = 5
-W_ENGINE = ["s", "s", "s", "s", "v", "sv", "sv"]
+W_ENGINE = ["s", "s", "s", "sv", "v", "sv", "sv"]
 BANKS = [(0, 1, 4, 5), (2, 3, 6), (7,)]
 
 
@@ -126,61 +126,92 @@ def tile_routed_moe_kernel(tc, xT, w, gate, offs, pos1, pos2, out):
         for q in range(len(BANKS)):
             for b in range(NB):
                 ps[(q, b)] = psum.tile([P, 4 * C], F32, name="ps%d_%d" % (q, b))
+        wg, wq, ws = [], [], []
         for e in range(E):
-            last = e == E - 1
-            wg = keep.tile([P, EW * PACK], BF16, name="wg%d" % e, align_bytes=64)
-            wq = keep.tile([P, EW], U32, name="wq%d" % e, align_bytes=64)
-            ws = keep.tile([P, EW], U8, name="ws%d" % e, align_bytes=64)
-            src = wraw[e][:].rearrange("p a (j c i) -> p a c j i", j=PACK, i=RUN)
-            dst = wg[:].rearrange("p (a c i j) -> p a c j i", a=PASSES, i=RUN, j=PACK)
-            if last:
-                move("v", dst[:, 0], src[:, 0])
-                move("v", dst[:, 1, 0:LAST_V // RUN], src[:, 1, 0:LAST_V // RUN])
-                move("s", dst[:, 1, LAST_V // RUN:N // RUN], src[:, 1, LAST_V // RUN:N // RUN])
-            elif len(W_ENGINE[e]) == PASSES:
-                for a in range(PASSES):
-                    move(W_ENGINE[e][a], dst[:, a], src[:, a])
-            else:
-                move(W_ENGINE[e], dst, src)
-            if last:
-                for c0, c1 in ((0, N), (N, N + P), (N + P, 2 * N)):
-                    nc.vector.quantize_mx(out=wq[:, c0:c1].bitcast(FP8X4), scales=ws[:, c0:c1],
-                                          in_=wg[:, c0 * PACK:c1 * PACK])
-            else:
-                nc.vector.quantize_mx(out=wq[:].bitcast(FP8X4), scales=ws[:], in_=wg[:])
-            q, i = bank_of[e]
-            for b in range(NB):
-                acc = ps[(q, b)][:, i * C:(i + 1) * C]
-                for a in range(PASSES):
-                    wc = slice(a * N + b * P, a * N + (b + 1) * P)
-                    xc = slice(e * C, (e + 1) * C)
-                    nc.tensor.matmul_mx(
-                        out=acc,
-                        lhsT=wq[:, wc].bitcast(FP8X4),
-                        lhsT_scale=ws[:, wc],
-                        rhs=xgq[a][:, xc].bitcast(FP8X4),
-                        rhs_scale=xgs[ROW0 * a:P, xc],
-                        start=(a == 0),
-                        stop=(a == PASSES - 1),
-                    )
-                if e == 5:
-                    nc.scalar.copy(out=y[b][:].rearrange("p (h q c) -> p h q c", h=2, q=2)[:, :, 0, :],
-                                   in_=ps[(0, b)][:].rearrange("p (h c) -> p h c", h=2))
-                elif e == 6:
-                    nc.scalar.copy(out=y[b][:, 2 * C:4 * C], in_=ps[(1, b)][:, 0:2 * C])
-                    nc.scalar.copy(out=y[b][:, 6 * C:7 * C], in_=ps[(1, b)][:, 2 * C:3 * C])
-                elif e == 7:
-                    move("v" if b == 0 else "s", y[b][:, 7 * C:8 * C], ps[(2, b)][:, 0:C])
+            wg.append(keep.tile([P, EW * PACK], BF16, name="wg%d" % e, align_bytes=64))
+            wq.append(keep.tile([P, EW], U32, name="wq%d" % e, align_bytes=64))
+            ws.append(keep.tile([P, EW], U8, name="ws%d" % e, align_bytes=64))
 
-        for b in range(NB):
-            t1 = keep.tile([P, T], F32, name="t1_%d" % b)
-            t2 = keep.tile([P, T], F32, name="t2_%d" % b)
-            o = keep.tile([P, T], F32, name="o_%d" % b)
-            nc.vector.tensor_tensor(out=t1[:], in0=y[b][:].indirect(pos1_t[:]), in1=g_t[(0, b)][:], op=MULT)
-            nc.vector.tensor_tensor(out=t2[:], in0=y[b][:].indirect(pos2_t[:]), in1=g_t[(1, b)][:], op=MULT)
-            nc.vector.tensor_add(out=o[:], in0=t1[:], in1=t2[:])
-            if b < NB - 1:
-                nc.sync.dma_start(out[b * P:(b + 1) * P, :], o[:])
+        def interleave(engine, e, a, c0, c1):
+            src = wraw[e][:].rearrange("p a (j c i) -> p a c j i", j=PACK, i=RUN)
+            dst = wg[e][:].rearrange("p (a c i j) -> p a c j i", a=PASSES, i=RUN, j=PACK)
+            if a is None:
+                move(engine, dst, src)
             else:
-                nc.sync.dma_start(out[b * P:(b + 1) * P, 0:T // 2], o[:, 0:T // 2])
-                nc.scalar.dma_start(out[b * P:(b + 1) * P, T // 2:T], o[:, T // 2:T])
+                move(engine, dst[:, a, c0 // RUN:c1 // RUN], src[:, a, c0 // RUN:c1 // RUN])
+
+        def quantize(e, c0, c1):
+            nc.vector.quantize_mx(out=wq[e][:, c0:c1].bitcast(FP8X4), scales=ws[e][:, c0:c1],
+                                  in_=wg[e][:, c0 * PACK:c1 * PACK])
+
+        def multiply(e, b):
+            q, i = bank_of[e]
+            for a in range(PASSES):
+                wc = slice(a * N + b * P, a * N + (b + 1) * P)
+                xc = slice(e * C, (e + 1) * C)
+                nc.tensor.matmul_mx(
+                    out=ps[(q, b)][:, i * C:(i + 1) * C],
+                    lhsT=wq[e][:, wc].bitcast(FP8X4),
+                    lhsT_scale=ws[e][:, wc],
+                    rhs=xgq[a][:, xc].bitcast(FP8X4),
+                    rhs_scale=xgs[ROW0 * a:P, xc],
+                    start=(a == 0),
+                    stop=(a == PASSES - 1),
+                )
+
+        def leave_psum(e, b):
+            if e == 5:
+                nc.scalar.copy(out=y[b][:].rearrange("p (h q c) -> p h q c", h=2, q=2)[:, :, 0, :],
+                               in_=ps[(0, b)][:].rearrange("p (h c) -> p h c", h=2))
+            elif e == 6:
+                nc.scalar.copy(out=y[b][:, 2 * C:4 * C], in_=ps[(1, b)][:, 0:2 * C])
+                nc.scalar.copy(out=y[b][:, 6 * C:7 * C], in_=ps[(1, b)][:, 2 * C:3 * C])
+            elif e == 7:
+                move("v" if b == 0 else "s", y[b][:, 7 * C:8 * C], ps[(2, b)][:, 0:C])
+
+        for e in range(E - 1):
+            if len(W_ENGINE[e]) == PASSES:
+                for a in range(PASSES):
+                    interleave(W_ENGINE[e][a], e, a, 0, N)
+            else:
+                interleave(W_ENGINE[e], e, None, 0, N)
+            quantize(e, 0, EW)
+            for b in range(NB):
+                multiply(e, b)
+                leave_psum(e, b)
+
+        t_ = {}
+        for b in range(NB):
+            for r in range(3):
+                t_[(r, b)] = keep.tile([P, T], F32, name="t%d_%d" % (r, b))
+        pos_t = [pos1_t, pos2_t]
+
+        def fetch(r, b):
+            nc.vector.tensor_tensor(out=t_[(r, b)][:], in0=y[b][:].indirect(pos_t[r][:]), in1=g_t[(r, b)][:], op=MULT)
+
+        def add(b, c0, c1):
+            nc.vector.tensor_add(out=t_[(2, b)][:, c0:c1], in0=t_[(0, b)][:, c0:c1], in1=t_[(1, b)][:, c0:c1])
+
+        def store(queue, b, c0, c1):
+            queue.dma_start(out[b * P:(b + 1) * P, c0:c1], t_[(2, b)][:, c0:c1])
+
+        L = E - 1
+        interleave("v", L, 0, 0, N)
+        quantize(L, 0, N)
+        interleave("v", L, 1, 0, P)
+        interleave("s", L, 1, P, N)
+        quantize(L, N, N + P)
+        multiply(L, 0)
+        leave_psum(L, 0)
+        fetch(0, 0)
+        quantize(L, N + P, 2 * N)
+        multiply(L, 1)
+        leave_psum(L, 1)
+        fetch(1, 0)
+        add(0, 0, T)
+        store(nc.sync, 0, 0, T)
+        fetch(0, 1)
+        fetch(1, 1)
+        add(1, 0, T)
+        store(nc.sync, 1, 0, T // 2)
+        store(nc.scalar, 1, T // 2, T)

@@ -1,6 +1,7 @@
 from contextlib import ExitStack
 
 import concourse.mybir as mybir
+from concourse.masks import make_identity
 
 K, T, E, C, N = 1024, 512, 8, 128, 256
 FLOPS = 2 * K * N * E * C
@@ -27,6 +28,7 @@ X_CHUNK = (512, 512)
 X0_V = 352
 LAST_V = 128
 EW = PASSES * N
+PE_ADD = 384
 FIRST_BY_PASS = 5
 W_ENGINE = ["s", "s", "s", "sv", "v", "sv", "sv"]
 BANKS = [(0, 1, 4, 5), (2, 3, 6), (7,)]
@@ -79,6 +81,9 @@ def tile_routed_moe_kernel(tc, xT, w, gate, offs, pos1, pos2, out):
                 t_ = keep.tile([P, T], F32, name="gate%d%d" % (r, b))
                 nc.sync.dma_start(t_[:], gate[r, b * P:(b + 1) * P, :])
                 g_t[(r, b)] = t_
+
+        ident = keep.tile([P, P], F32, name="ident")
+        make_identity(nc, ident[:])
 
         warm = keep.tile([P, 1], F32, name="warm")
         nc.vector.memset(warm[:], 0.0)
@@ -203,12 +208,16 @@ def tile_routed_moe_kernel(tc, xT, w, gate, offs, pos1, pos2, out):
         quantize(L, N, N + P)
         multiply(L, 0)
         leave_psum(L, 0)
+        pa = psum.tile([P, T], F32, name="pa")
         fetch(0, 0)
         quantize(L, N + P, 2 * N)
         multiply(L, 1)
         leave_psum(L, 1)
+        nc.tensor.matmul(pa[:, 0:PE_ADD], lhsT=ident[:], rhs=t_[(0, 0)][:, 0:PE_ADD], start=True, stop=False)
         fetch(1, 0)
-        add(0, 0, T)
+        nc.tensor.matmul(pa[:, 0:PE_ADD], lhsT=ident[:], rhs=t_[(1, 0)][:, 0:PE_ADD], start=False, stop=True)
+        nc.scalar.copy(out=t_[(2, 0)][:, 0:PE_ADD], in_=pa[:, 0:PE_ADD])
+        add(0, PE_ADD, T)
         store(nc.sync, 0, 0, T)
         fetch(0, 1)
         fetch(1, 1)

@@ -28,9 +28,10 @@ X_CHUNK = (512, 512)
 X0_V = 352
 LAST_V = 128
 EW = PASSES * N
+G_COLS = 128
 PE_ADD = 384
 FIRST_BY_PASS = 5
-W_ENGINE = ["s", "s", "s", "sv", "v", "sv", "sv"]
+W_ENGINE = ["gg", "s", "s", "s", "sv", "sv", "sv"]
 BANKS = [(0, 1, 4, 5), (2, 3, 6), (7,)]
 
 
@@ -177,7 +178,8 @@ def tile_routed_moe_kernel(tc, xT, w, gate, offs, pos1, pos2, out):
         for e in range(E - 1):
             if len(W_ENGINE[e]) == PASSES:
                 for a in range(PASSES):
-                    interleave(W_ENGINE[e][a], e, a, 0, N)
+                    for c0 in range(0, N, G_COLS if W_ENGINE[e][a] == "g" else N):
+                        interleave(W_ENGINE[e][a], e, a, c0, c0 + (G_COLS if W_ENGINE[e][a] == "g" else N))
             else:
                 interleave(W_ENGINE[e], e, None, 0, N)
             quantize(e, 0, EW)

@@ -20,6 +20,7 @@ P = 128
 PACK = 4
 ROW0 = 4
 RUN = 4
+DMA_ALIGN = 256
 PASSES = K // (P * PACK)
 NB = N // P
 SLOTS = E * C
@@ -59,14 +60,14 @@ def tile_routed_moe_kernel(tc, xT, w, gate, offs, pos1, pos2, out):
         xraw = {}
         for a in range(PASSES):
             for c in range(T // X_CHUNK[a]):
-                t_ = keep.tile([P, PACK, X_CHUNK[a]], F32, name="xraw%d_%d" % (a, c))
+                t_ = keep.tile([P, PACK, X_CHUNK[a]], F32, name="xraw%d_%d" % (a, c), align_bytes=DMA_ALIGN)
                 nc.sync.dma_start(t_[:], x_view[a, :, :, c * X_CHUNK[a]:(c + 1) * X_CHUNK[a]])
                 xraw[(a, c)] = t_
             if a == 0:
                 nc.sync.dma_start(offs_t[:], offs)
         wraw = []
         for e in range(E):
-            t_ = keep.tile([P, PASSES, PACK * N], F32, name="wraw%d" % e)
+            t_ = keep.tile([P, PASSES, PACK * N], F32, name="wraw%d" % e, align_bytes=DMA_ALIGN)
             src = w[e].rearrange("(a p j) n -> p a (j n)", p=P, j=PACK)
             if e < FIRST_BY_PASS:
                 nc.sync.dma_start(t_[:], src)
@@ -79,7 +80,7 @@ def tile_routed_moe_kernel(tc, xT, w, gate, offs, pos1, pos2, out):
         g_t = {}
         for b in range(NB):
             for r in range(2):
-                t_ = keep.tile([P, T], F32, name="gate%d%d" % (r, b))
+                t_ = keep.tile([P, T], F32, name="gate%d%d" % (r, b), align_bytes=DMA_ALIGN)
                 nc.sync.dma_start(t_[:], gate[r, b * P:(b + 1) * P, :])
                 g_t[(r, b)] = t_
 
@@ -190,7 +191,7 @@ def tile_routed_moe_kernel(tc, xT, w, gate, offs, pos1, pos2, out):
         t_ = {}
         for b in range(NB):
             for r in range(3):
-                t_[(r, b)] = keep.tile([P, T], F32, name="t%d_%d" % (r, b))
+                t_[(r, b)] = keep.tile([P, T], F32, name="t%d_%d" % (r, b), align_bytes=DMA_ALIGN)
         pos_t = [pos1_t, pos2_t]
 
         def fetch(r, b):

@@ -1,7 +1,6 @@
 from contextlib import ExitStack
 
 import concourse.mybir as mybir
-from concourse.masks import make_identity
 
 K, T, E, C, N = 1024, 512, 8, 128, 256
 FLOPS = 2 * K * N * E * C
@@ -25,14 +24,12 @@ PASSES = K // (P * PACK)
 NB = N // P
 SLOTS = E * C
 WIN = 2 * SLOTS
-X_CHUNK = (512, 512)
 X0_V = 352
-LAST_V = 128
-EW = PASSES * N
-G_COLS = 128
-PE_ADD = 384
+WHOLE = 6
 FIRST_BY_PASS = 5
-W_ENGINE = ["gg", "s", "s", "s", "sv", "sv", "sv"]
+G_COLS = 128
+W_ENGINE = ["gg", "ss", "ss", "sv", "sv", "sv"]
+B_ENGINE = {(6, 0): "ss", (7, 0): "vv", (6, 1): "ss", (7, 1): "sv"}
 BANKS = [(0, 1, 4, 5), (2, 3, 6), (7,)]
 
 
@@ -57,16 +54,15 @@ def tile_routed_moe_kernel(tc, xT, w, gate, offs, pos1, pos2, out):
         pos2_t = lists.tile([P, T // 16], U16, name="pos2_t")
 
         x_view = xT.rearrange("(a p j) t -> a p j t", p=P, j=PACK)
-        xraw = {}
+        xraw = []
         for a in range(PASSES):
-            for c in range(T // X_CHUNK[a]):
-                t_ = keep.tile([P, PACK, X_CHUNK[a]], F32, name="xraw%d_%d" % (a, c), align_bytes=DMA_ALIGN)
-                nc.sync.dma_start(t_[:], x_view[a, :, :, c * X_CHUNK[a]:(c + 1) * X_CHUNK[a]])
-                xraw[(a, c)] = t_
+            t_ = keep.tile([P, PACK, T], F32, name="xraw%d" % a, align_bytes=DMA_ALIGN)
+            nc.sync.dma_start(t_[:], x_view[a])
+            xraw.append(t_)
             if a == 0:
                 nc.sync.dma_start(offs_t[:], offs)
-        wraw = []
-        for e in range(E):
+        wraw = {}
+        for e in range(WHOLE):
             t_ = keep.tile([P, PASSES, PACK * N], F32, name="wraw%d" % e, align_bytes=DMA_ALIGN)
             src = w[e].rearrange("(a p j) n -> p a (j n)", p=P, j=PACK)
             if e < FIRST_BY_PASS:
@@ -74,18 +70,31 @@ def tile_routed_moe_kernel(tc, xT, w, gate, offs, pos1, pos2, out):
             else:
                 for a in range(PASSES):
                     nc.sync.dma_start(t_[:, a, :], src[:, a, :])
-            wraw.append(t_)
+            wraw[e] = t_
+        g_t = {}
+
+        def load_block(e, b):
+            t_ = keep.tile([P, PASSES, PACK, P], F32, name="wraw%d_%d" % (e, b), align_bytes=DMA_ALIGN)
+            src = w[e].rearrange("(a p j) n -> a p j n", p=P, j=PACK)
+            for a in range(PASSES):
+                nc.sync.dma_start(t_[:, a, :, :], src[a, :, :, b * P:(b + 1) * P])
+            wraw[(e, b)] = t_
+
+        def load_gate(r, b):
+            t_ = keep.tile([P, T], F32, name="gate%d%d" % (r, b), align_bytes=DMA_ALIGN)
+            nc.sync.dma_start(t_[:], gate[r, b * P:(b + 1) * P, :])
+            g_t[(r, b)] = t_
+
+        load_block(6, 0)
+        load_block(7, 0)
         nc.sync.dma_start(pos1_t[:], pos1)
         nc.sync.dma_start(pos2_t[:], pos2)
-        g_t = {}
-        for b in range(NB):
-            for r in range(2):
-                t_ = keep.tile([P, T], F32, name="gate%d%d" % (r, b), align_bytes=DMA_ALIGN)
-                nc.sync.dma_start(t_[:], gate[r, b * P:(b + 1) * P, :])
-                g_t[(r, b)] = t_
-
-        ident = keep.tile([P, P], F32, name="ident")
-        make_identity(nc, ident[:])
+        load_gate(0, 0)
+        load_block(6, 1)
+        load_block(7, 1)
+        load_gate(1, 0)
+        load_gate(0, 1)
+        load_gate(1, 1)
 
         warm = keep.tile([P, 1], F32, name="warm")
         nc.vector.memset(warm[:], 0.0)
@@ -102,20 +111,12 @@ def tile_routed_moe_kernel(tc, xT, w, gate, offs, pos1, pos2, out):
         for a in range(PASSES):
             xg = keep.tile([P, T * PACK], BF16, name="xg%d" % a, align_bytes=64)
             dst = xg[:].rearrange("p (c i j) -> p c j i", i=RUN, j=PACK)
-            XCH = X_CHUNK[a]
-            for c in range(T // XCH):
-                src = xraw[(a, c)][:].rearrange("p j (c i) -> p c j i", i=RUN)
-                c0 = c * XCH // RUN
-                v = X0_V if a == 0 else 0
-                if v:
-                    nc.vector.tensor_copy(out=dst[:, c0:c0 + v // RUN], in_=src[:, 0:v // RUN])
-                nc.scalar.copy(out=dst[:, c0 + v // RUN:c0 + XCH // RUN], in_=src[:, v // RUN:XCH // RUN])
-                if a == 0:
-                    tc_ = slice(c * XCH, (c + 1) * XCH)
-                    nc.vector.quantize_mx(out=xq[a][:, tc_].bitcast(FP8X4), scales=xsc[ROW0 * a:P, tc_],
-                                          in_=xg[:, c * XCH * PACK:(c + 1) * XCH * PACK])
-            if a > 0:
-                nc.vector.quantize_mx(out=xq[a][:, 0:T].bitcast(FP8X4), scales=xsc[ROW0 * a:P, 0:T], in_=xg[:])
+            src = xraw[a][:].rearrange("p j (c i) -> p c j i", i=RUN)
+            v = X0_V // RUN if a == 0 else 0
+            if v:
+                nc.vector.tensor_copy(out=dst[:, 0:v], in_=src[:, 0:v])
+            nc.scalar.copy(out=dst[:, v:], in_=src[:, v:])
+            nc.vector.quantize_mx(out=xq[a][:, 0:T].bitcast(FP8X4), scales=xsc[ROW0 * a:P, 0:T], in_=xg[:])
 
         xgq = [keep.tile([P, SLOTS], U32, name="xgq%d" % a, align_bytes=64) for a in range(PASSES)]
         xgs = keep.tile([P, SLOTS], U8, name="xgs", align_bytes=64)
@@ -133,60 +134,69 @@ def tile_routed_moe_kernel(tc, xT, w, gate, offs, pos1, pos2, out):
         for q in range(len(BANKS)):
             for b in range(NB):
                 ps[(q, b)] = psum.tile([P, 4 * C], F32, name="ps%d_%d" % (q, b))
-        wg, wq, ws = [], [], []
-        for e in range(E):
-            wg.append(keep.tile([P, EW * PACK], BF16, name="wg%d" % e, align_bytes=64))
-            wq.append(keep.tile([P, EW], U32, name="wq%d" % e, align_bytes=64))
-            ws.append(keep.tile([P, EW], U8, name="ws%d" % e, align_bytes=64))
 
-        def interleave(engine, e, a, c0, c1):
-            src = wraw[e][:].rearrange("p a (j c i) -> p a c j i", j=PACK, i=RUN)
-            dst = wg[e][:].rearrange("p (a c i j) -> p a c j i", a=PASSES, i=RUN, j=PACK)
-            if a is None:
-                move(engine, dst, src)
-            else:
-                move(engine, dst[:, a, c0 // RUN:c1 // RUN], src[:, a, c0 // RUN:c1 // RUN])
-
-        def quantize(e, c0, c1):
-            nc.vector.quantize_mx(out=wq[e][:, c0:c1].bitcast(FP8X4), scales=ws[e][:, c0:c1],
-                                  in_=wg[e][:, c0 * PACK:c1 * PACK])
-
-        def multiply(e, b):
+        def multiply(e, b, codes, scales, cols):
             q, i = bank_of[e]
             for a in range(PASSES):
-                wc = slice(a * N + b * P, a * N + (b + 1) * P)
+                wc = slice(cols[a], cols[a] + P)
                 xc = slice(e * C, (e + 1) * C)
                 nc.tensor.matmul_mx(
                     out=ps[(q, b)][:, i * C:(i + 1) * C],
-                    lhsT=wq[e][:, wc].bitcast(FP8X4),
-                    lhsT_scale=ws[e][:, wc],
+                    lhsT=codes[:, wc].bitcast(FP8X4),
+                    lhsT_scale=scales[:, wc],
                     rhs=xgq[a][:, xc].bitcast(FP8X4),
                     rhs_scale=xgs[ROW0 * a:P, xc],
                     start=(a == 0),
                     stop=(a == PASSES - 1),
                 )
 
-        def leave_psum(e, b):
-            if e == 5:
-                nc.scalar.copy(out=y[b][:].rearrange("p (h q c) -> p h q c", h=2, q=2)[:, :, 0, :],
-                               in_=ps[(0, b)][:].rearrange("p (h c) -> p h c", h=2))
-            elif e == 6:
-                nc.scalar.copy(out=y[b][:, 2 * C:4 * C], in_=ps[(1, b)][:, 0:2 * C])
-                nc.scalar.copy(out=y[b][:, 6 * C:7 * C], in_=ps[(1, b)][:, 2 * C:3 * C])
-            elif e == 7:
-                move("v" if b == 0 else "s", y[b][:, 7 * C:8 * C], ps[(2, b)][:, 0:C])
-
-        for e in range(E - 1):
-            if len(W_ENGINE[e]) == PASSES:
-                for a in range(PASSES):
-                    for c0 in range(0, N, G_COLS if W_ENGINE[e][a] == "g" else N):
-                        interleave(W_ENGINE[e][a], e, a, c0, c0 + (G_COLS if W_ENGINE[e][a] == "g" else N))
+        def leave_psum(engine, q, b):
+            experts = BANKS[q]
+            if len(experts) == 4:
+                move(engine, y[b][:].rearrange("p (h q c) -> p h q c", h=2, q=2)[:, :, 0, :],
+                     ps[(q, b)][:].rearrange("p (h c) -> p h c", h=2))
             else:
-                interleave(W_ENGINE[e], e, None, 0, N)
-            quantize(e, 0, EW)
+                pairs = len(experts) // 2 * 2
+                for i, n in ((0, pairs), (pairs, len(experts) - pairs)):
+                    if n:
+                        e0 = experts[i]
+                        move(engine, y[b][:, e0 * C:(e0 + n) * C], ps[(q, b)][:, i * C:(i + n) * C])
+
+        for e in range(WHOLE):
+            wg = keep.tile([P, PASSES * N * PACK], BF16, name="wg%d" % e, align_bytes=64)
+            wq = keep.tile([P, PASSES * N], U32, name="wq%d" % e, align_bytes=64)
+            ws = keep.tile([P, PASSES * N], U8, name="ws%d" % e, align_bytes=64)
+            src = wraw[e][:].rearrange("p a (j c i) -> p a c j i", j=PACK, i=RUN)
+            dst = wg[:].rearrange("p (a c i j) -> p a c j i", a=PASSES, i=RUN, j=PACK)
+            if W_ENGINE[e] == "ss":
+                move("s", dst, src)
+            else:
+                for a in range(PASSES):
+                    step = (G_COLS if W_ENGINE[e][a] == "g" else N) // RUN
+                    for c0 in range(0, N // RUN, step):
+                        move(W_ENGINE[e][a], dst[:, a, c0:c0 + step], src[:, a, c0:c0 + step])
+            nc.vector.quantize_mx(out=wq[:].bitcast(FP8X4), scales=ws[:], in_=wg[:])
             for b in range(NB):
-                multiply(e, b)
-                leave_psum(e, b)
+                multiply(e, b, wq, ws, [a * N + b * P for a in range(PASSES)])
+            if e == BANKS[0][-1]:
+                for b in range(NB):
+                    leave_psum("s", 0, b)
+
+        def block(e, b, by_pass):
+            wg = keep.tile([P, PASSES * P * PACK], BF16, name="wg%d_%d" % (e, b), align_bytes=64)
+            wq = keep.tile([P, PASSES * P], U32, name="wq%d_%d" % (e, b), align_bytes=64)
+            ws = keep.tile([P, PASSES * P], U8, name="ws%d_%d" % (e, b), align_bytes=64)
+            src = wraw[(e, b)][:].rearrange("p a j (c i) -> p a c j i", i=RUN)
+            dst = wg[:].rearrange("p (a c i j) -> p a c j i", a=PASSES, i=RUN, j=PACK)
+            half = P * PACK
+            for a in range(PASSES):
+                move(B_ENGINE[(e, b)][a], dst[:, a], src[:, a])
+                if by_pass:
+                    nc.vector.quantize_mx(out=wq[:, a * P:(a + 1) * P].bitcast(FP8X4), scales=ws[:, a * P:(a + 1) * P],
+                                          in_=wg[:, a * half:(a + 1) * half])
+            if not by_pass:
+                nc.vector.quantize_mx(out=wq[:].bitcast(FP8X4), scales=ws[:], in_=wg[:])
+            multiply(e, b, wq, ws, [a * P for a in range(PASSES)])
 
         t_ = {}
         for b in range(NB):
@@ -203,24 +213,17 @@ def tile_routed_moe_kernel(tc, xT, w, gate, offs, pos1, pos2, out):
         def store(queue, b, c0, c1):
             queue.dma_start(out[b * P:(b + 1) * P, c0:c1], t_[(2, b)][:, c0:c1])
 
-        L = E - 1
-        interleave("v", L, 0, 0, N)
-        quantize(L, 0, N)
-        interleave("v", L, 1, 0, P)
-        interleave("s", L, 1, P, N)
-        quantize(L, N, N + P)
-        multiply(L, 0)
-        leave_psum(L, 0)
-        pa = psum.tile([P, T], F32, name="pa")
+        block(6, 0, False)
+        leave_psum("s", 1, 0)
+        block(7, 0, True)
+        leave_psum("v", 2, 0)
         fetch(0, 0)
-        quantize(L, N + P, 2 * N)
-        multiply(L, 1)
-        leave_psum(L, 1)
-        nc.tensor.matmul(pa[:, 0:PE_ADD], lhsT=ident[:], rhs=t_[(0, 0)][:, 0:PE_ADD], start=True, stop=False)
+        block(6, 1, False)
+        leave_psum("s", 1, 1)
         fetch(1, 0)
-        nc.tensor.matmul(pa[:, 0:PE_ADD], lhsT=ident[:], rhs=t_[(1, 0)][:, 0:PE_ADD], start=False, stop=True)
-        nc.scalar.copy(out=t_[(2, 0)][:, 0:PE_ADD], in_=pa[:, 0:PE_ADD])
-        add(0, PE_ADD, T)
+        block(7, 1, True)
+        leave_psum("s", 2, 1)
+        add(0, 0, T)
         store(nc.sync, 0, 0, T)
         fetch(0, 1)
         fetch(1, 1)

from contextlib import ExitStack

import concourse.mybir as mybir

K, T, E, C, N = 1024, 512, 8, 128, 256
FLOPS = 2 * K * N * E * C

F32 = mybir.dt.float32
BF16 = mybir.dt.bfloat16
I32 = mybir.dt.int32
U32 = mybir.dt.uint32
U16 = mybir.dt.uint16
U8 = mybir.dt.uint8
FP8X4 = mybir.dt.float8_e4m3fn_x4
MULT = mybir.AluOpType.mult
ADD = mybir.AluOpType.add

P = 128
PACK = 4
ROW0 = 4
RUN = 4
DMA_ALIGN = 256
PASSES = K // (P * PACK)
NB = N // P
SLOTS = E * C
WIN = 2 * SLOTS
X0_V = 352
WHOLE = 6
FIRST_BY_PASS = 5
G_COLS = 128
W_ENGINE = ["gg", "ss", "ss", "sv", "sv", "sv"]
B_ENGINE = {(6, 0): "ss", (7, 0): "vv", (6, 1): "ss", (7, 1): "sv"}
BANKS = [(0, 1, 4, 5), (2, 3, 6), (7,)]


def tile_routed_moe_kernel(tc, xT, w, gate, offs, pos1, pos2, out):
    nc = tc.nc

    def move(engine, dst, src):
        if engine == "s":
            nc.scalar.copy(out=dst, in_=src)
        elif engine == "v":
            nc.vector.tensor_copy(out=dst, in_=src)
        else:
            nc.gpsimd.tensor_scalar(out=dst, in0=src, scalar1=1.0, scalar2=0.0, op0=MULT, op1=ADD)

    with ExitStack() as ctx:
        lists = ctx.enter_context(tc.tile_pool(name="lists", bufs=1))
        keep = ctx.enter_context(tc.tile_pool(name="keep", bufs=1))
        psum = ctx.enter_context(tc.psum_pool(name="psum", bufs=1))

        offs_t = lists.tile([P, SLOTS // 16], U16, name="offs_t")
        pos1_t = lists.tile([P, T // 16], U16, name="pos1_t")
        pos2_t = lists.tile([P, T // 16], U16, name="pos2_t")

        x_view = xT.rearrange("(a p j) t -> a p j t", p=P, j=PACK)
        xraw = []
        for a in range(PASSES):
            t_ = keep.tile([P, PACK, T], F32, name="xraw%d" % a, align_bytes=DMA_ALIGN)
            nc.sync.dma_start(t_[:], x_view[a])
            xraw.append(t_)
            if a == 0:
                nc.sync.dma_start(offs_t[:], offs)
        wraw = {}
        for e in range(WHOLE):
            t_ = keep.tile([P, PASSES, PACK * N], F32, name="wraw%d" % e, align_bytes=DMA_ALIGN)
            src = w[e].rearrange("(a p j) n -> p a (j n)", p=P, j=PACK)
            if e < FIRST_BY_PASS:
                nc.sync.dma_start(t_[:], src)
            else:
                for a in range(PASSES):
                    nc.sync.dma_start(t_[:, a, :], src[:, a, :])
            wraw[e] = t_
        g_t = {}

        def load_block(e, b):
            t_ = keep.tile([P, PASSES, PACK, P], F32, name="wraw%d_%d" % (e, b), align_bytes=DMA_ALIGN)
            src = w[e].rearrange("(a p j) n -> a p j n", p=P, j=PACK)
            for a in range(PASSES):
                nc.sync.dma_start(t_[:, a, :, :], src[a, :, :, b * P:(b + 1) * P])
            wraw[(e, b)] = t_

        def load_gate(r, b):
            t_ = keep.tile([P, T], F32, name="gate%d%d" % (r, b), align_bytes=DMA_ALIGN)
            nc.sync.dma_start(t_[:], gate[r, b * P:(b + 1) * P, :])
            g_t[(r, b)] = t_

        load_block(6, 0)
        load_block(7, 0)
        nc.sync.dma_start(pos1_t[:], pos1)
        nc.sync.dma_start(pos2_t[:], pos2)
        load_gate(0, 0)
        load_block(6, 1)
        load_block(7, 1)
        load_gate(1, 0)
        load_gate(0, 1)
        load_gate(1, 1)

        warm = keep.tile([P, 1], F32, name="warm")
        nc.vector.memset(warm[:], 0.0)
        warm2 = keep.tile([P, 1], F32, name="warm2")
        nc.scalar.copy(warm2[:], warm[:])

        xq = []
        xsc = keep.tile([P, WIN], U8, name="xsc", align_bytes=64)
        nc.vector.memset(xsc[:].bitcast(I32), 0)
        for a in range(PASSES):
            q = keep.tile([P, WIN], I32, name="xq%d" % a, align_bytes=64)
            nc.vector.memset(q[:, T:WIN], 0)
            xq.append(q)
        for a in range(PASSES):
            xg = keep.tile([P, T * PACK], BF16, name="xg%d" % a, align_bytes=64)
            dst = xg[:].rearrange("p (c i j) -> p c j i", i=RUN, j=PACK)
            src = xraw[a][:].rearrange("p j (c i) -> p c j i", i=RUN)
            v = X0_V // RUN if a == 0 else 0
            if v:
                nc.vector.tensor_copy(out=dst[:, 0:v], in_=src[:, 0:v])
            nc.scalar.copy(out=dst[:, v:], in_=src[:, v:])
            nc.vector.quantize_mx(out=xq[a][:, 0:T].bitcast(FP8X4), scales=xsc[ROW0 * a:P, 0:T], in_=xg[:])

        xgq = [keep.tile([P, SLOTS], U32, name="xgq%d" % a, align_bytes=64) for a in range(PASSES)]
        xgs = keep.tile([P, SLOTS], U8, name="xgs", align_bytes=64)
        y = [keep.tile([P, SLOTS], F32, name="y%d" % b) for b in range(NB)]

        nc.vector.tensor_copy(out=xgq[0][:], in_=xq[0][:].bitcast(U32).indirect(offs_t[:]))
        nc.vector.tensor_copy(out=xgs[:], in_=xsc[:].indirect(offs_t[:]))
        nc.vector.tensor_copy(out=xgq[1][:], in_=xq[1][:].bitcast(U32).indirect(offs_t[:]))

        bank_of = {}
        for q, experts in enumerate(BANKS):
            for i, e in enumerate(experts):
                bank_of[e] = (q, i)
        ps = {}
        for q in range(len(BANKS)):
            for b in range(NB):
                ps[(q, b)] = psum.tile([P, 4 * C], F32, name="ps%d_%d" % (q, b))

        def multiply(e, b, codes, scales, cols):
            q, i = bank_of[e]
            for a in range(PASSES):
                wc = slice(cols[a], cols[a] + P)
                xc = slice(e * C, (e + 1) * C)
                nc.tensor.matmul_mx(
                    out=ps[(q, b)][:, i * C:(i + 1) * C],
                    lhsT=codes[:, wc].bitcast(FP8X4),
                    lhsT_scale=scales[:, wc],
                    rhs=xgq[a][:, xc].bitcast(FP8X4),
                    rhs_scale=xgs[ROW0 * a:P, xc],
                    start=(a == 0),
                    stop=(a == PASSES - 1),
                )

        def leave_psum(engine, q, b):
            experts = BANKS[q]
            if len(experts) == 4:
                move(engine, y[b][:].rearrange("p (h q c) -> p h q c", h=2, q=2)[:, :, 0, :],
                     ps[(q, b)][:].rearrange("p (h c) -> p h c", h=2))
            else:
                pairs = len(experts) // 2 * 2
                for i, n in ((0, pairs), (pairs, len(experts) - pairs)):
                    if n:
                        e0 = experts[i]
                        move(engine, y[b][:, e0 * C:(e0 + n) * C], ps[(q, b)][:, i * C:(i + n) * C])

        for e in range(WHOLE):
            wg = keep.tile([P, PASSES * N * PACK], BF16, name="wg%d" % e, align_bytes=64)
            wq = keep.tile([P, PASSES * N], U32, name="wq%d" % e, align_bytes=64)
            ws = keep.tile([P, PASSES * N], U8, name="ws%d" % e, align_bytes=64)
            src = wraw[e][:].rearrange("p a (j c i) -> p a c j i", j=PACK, i=RUN)
            dst = wg[:].rearrange("p (a c i j) -> p a c j i", a=PASSES, i=RUN, j=PACK)
            if W_ENGINE[e] == "ss":
                move("s", dst, src)
            else:
                for a in range(PASSES):
                    step = (G_COLS if W_ENGINE[e][a] == "g" else N) // RUN
                    for c0 in range(0, N // RUN, step):
                        move(W_ENGINE[e][a], dst[:, a, c0:c0 + step], src[:, a, c0:c0 + step])
            nc.vector.quantize_mx(out=wq[:].bitcast(FP8X4), scales=ws[:], in_=wg[:])
            for b in range(NB):
                multiply(e, b, wq, ws, [a * N + b * P for a in range(PASSES)])
            if e == BANKS[0][-1]:
                for b in range(NB):
                    leave_psum("s", 0, b)

        def block(e, b, by_pass):
            wg = keep.tile([P, PASSES * P * PACK], BF16, name="wg%d_%d" % (e, b), align_bytes=64)
            wq = keep.tile([P, PASSES * P], U32, name="wq%d_%d" % (e, b), align_bytes=64)
            ws = keep.tile([P, PASSES * P], U8, name="ws%d_%d" % (e, b), align_bytes=64)
            src = wraw[(e, b)][:].rearrange("p a j (c i) -> p a c j i", i=RUN)
            dst = wg[:].rearrange("p (a c i j) -> p a c j i", a=PASSES, i=RUN, j=PACK)
            half = P * PACK
            for a in range(PASSES):
                move(B_ENGINE[(e, b)][a], dst[:, a], src[:, a])
                if by_pass:
                    nc.vector.quantize_mx(out=wq[:, a * P:(a + 1) * P].bitcast(FP8X4), scales=ws[:, a * P:(a + 1) * P],
                                          in_=wg[:, a * half:(a + 1) * half])
            if not by_pass:
                nc.vector.quantize_mx(out=wq[:].bitcast(FP8X4), scales=ws[:], in_=wg[:])
            multiply(e, b, wq, ws, [a * P for a in range(PASSES)])

        t_ = {}
        for b in range(NB):
            for r in range(3):
                t_[(r, b)] = keep.tile([P, T], F32, name="t%d_%d" % (r, b), align_bytes=DMA_ALIGN)
        pos_t = [pos1_t, pos2_t]

        def fetch(r, b):
            nc.vector.tensor_tensor(out=t_[(r, b)][:], in0=y[b][:].indirect(pos_t[r][:]), in1=g_t[(r, b)][:], op=MULT)

        def add(b, c0, c1):
            nc.vector.tensor_add(out=t_[(2, b)][:, c0:c1], in0=t_[(0, b)][:, c0:c1], in1=t_[(1, b)][:, c0:c1])

        def store(queue, b, c0, c1):
            queue.dma_start(out[b * P:(b + 1) * P, c0:c1], t_[(2, b)][:, c0:c1])

        block(6, 0, False)
        leave_psum("s", 1, 0)
        block(7, 0, True)
        leave_psum("v", 2, 0)
        fetch(0, 0)
        block(6, 1, False)
        leave_psum("s", 1, 1)
        fetch(1, 0)
        block(7, 1, True)
        leave_psum("s", 2, 1)
        add(0, 0, T)
        store(nc.sync, 0, 0, T)
        fetch(0, 1)
        fetch(1, 1)
        add(1, 0, T)
        store(nc.sync, 1, 0, T // 2)
        store(nc.scalar, 1, T // 2, T)
